import numpy as np
import ml_dtypes


def mxq(x, axis, fmt="e4m3"):
    dtype, down = {"e4m3": (ml_dtypes.float8_e4m3fn, 7), "e5m2": (ml_dtypes.float8_e5m2, 14)}[fmt]
    v = np.moveaxis(np.asarray(x, np.float32).astype(ml_dtypes.bfloat16).astype(np.float64), axis, -1)
    blocks = v.reshape(v.shape[:-1] + (-1, 32))
    amax = np.abs(blocks).max(-1, keepdims=True)
    byte = np.maximum(np.where(amax > 0, np.frexp(amax)[1] - 1 + 127, 0) - down, 1)
    scale = np.exp2(byte - 127.0)
    codes = (blocks / scale).astype(np.float32).astype(dtype).astype(np.float64)
    return np.moveaxis((codes * scale).reshape(v.shape), -1, axis)


WIDE = False


def mx_kscale(k):
    if not WIDE:
        return np.ones(k)
    levels = np.array([10, -10, 5, -5, 0])
    if k % 512:
        return np.exp2(np.random.permutation(np.resize(levels, k // 32))).repeat(32)
    a = np.empty((k // 512, 16))
    for p in range(k // 512):
        a[p, :8] = np.random.permutation(np.resize(levels, 8))
        for g in range(8):
            far = levels[np.abs(levels - a[p, g]) >= 10]
            a[p, g + 8] = far[np.random.randint(len(far))]
    return np.exp2(a.ravel()).repeat(32)


def f64(x):
    return np.asarray(x).astype(np.float64)


def striped8(idx):
    return np.concatenate([v.reshape(-1, 16).T for v in idx]).astype(np.uint16)


def unstriped8(offs):
    return np.stack([offs[16 * g:16 * g + 16].T.reshape(-1) for g in range(8)]).astype(np.int64)


E2M1 = np.array([0.0, 0.5, 1.0, 1.5, 2.0, 3.0, 4.0, 6.0, -0.0, -0.5, -1.0, -1.5, -2.0, -3.0, -4.0, -6.0])


def pack_weight(w, fmt):
    k, n = w.shape
    w = f64(np.asarray(w, np.float32).astype(ml_dtypes.bfloat16)).reshape(k // 32, 32, n)
    amax = np.abs(w).max(1)
    if fmt == "e4m3":
        byte = np.frexp(amax)[1] - 1 + 127 - 7
    else:
        mant, ex = np.frexp(amax / 6.0)
        byte = np.where(mant > 0.5, ex, ex - 1) + 127
    byte = np.clip(np.where(amax > 0, byte, 1), 1, 254)
    scaled = (w * np.exp2(127.0 - byte)[:, None, :]).reshape(k, n).astype(np.float32)
    by_word = np.ascontiguousarray(scaled.reshape(k // 512, 128, 4, n).transpose(0, 1, 3, 2))
    if fmt == "e4m3":
        words = by_word.astype(ml_dtypes.float8_e4m3fn).view(np.uint8)
    else:
        c = by_word.astype(ml_dtypes.float4_e2m1fn).view(np.uint8) & 0xF
        words = (c[..., 0::2] | (c[..., 1::2] << 4)).reshape(k // 512, 128, 2 * n)
    return np.ascontiguousarray(words), np.ascontiguousarray(byte.astype(np.uint8).reshape(k // 512, 16, n))


def unpack_weight(words, scales, fmt):
    g, _, n = scales.shape
    words = np.ascontiguousarray(words).reshape(g, 128, n, -1)
    if fmt == "e4m3":
        vals = words.view(ml_dtypes.float8_e4m3fn).astype(np.float64)
    else:
        nib = np.empty((g, 128, n, 4), np.uint8)
        nib[..., 0::2] = words & 0xF
        nib[..., 1::2] = words >> 4
        vals = E2M1[nib]
    vals = vals * np.repeat(np.exp2(scales.astype(np.float64) - 127.0), 8, axis=1)[..., None]
    return vals.transpose(0, 1, 3, 2).reshape(g * 512, n)


K, M, T, S = 512, 512, 1024, 512


def setup_inputs():
    n = np.random.standard_normal
    s = mx_kscale(K)[:, None]
    p_w = pack_weight(n((K, M)) / np.sqrt(K) / s, "e4m3")
    return {
        "xT": (n((K, T)) * s).astype(np.float32),
        "w_words": p_w[0],
        "w_scales": p_w[1],
        "wgt": np.repeat(np.random.uniform(0.5, 2.0, (8, S)), 16, axis=0).astype(np.float32),
        "wgo": np.repeat(np.random.uniform(0.5, 2.0, (8, S)), 16, axis=0).astype(np.float32),
        "offs": striped8(np.stack([np.random.permutation(T)[:S] for _ in range(8)])),
        "offs2": striped8(np.stack([np.random.permutation(T)[:S] for _ in range(8)])),
    }


def reference(xT, w_words, w_scales, wgt, wgo, offs, offs2):
    idx = unstriped8(offs)
    group = np.arange(K) % 512 // 64
    xg = f64(wgt)[np.arange(K) // 4 % 128] * f64(xT)[np.arange(K)[:, None], idx[group]]
    xT_ = mxq(xg, 0, "e4m3")
    w_ = unpack_weight(w_words, w_scales, "e4m3")
    y = w_.T @ xT_
    place = unstriped8(offs2)[np.arange(M) % 128 // 16]
    out = np.zeros((M, T))
    out[np.arange(M)[:, None], place] = f64(wgo)[np.arange(M) % 128] * (y)
    return out

@@ -1,0 +1,126 @@
+from contextlib import ExitStack
+
+import concourse.mybir as mybir
+
+K, M, T, S = 512, 512, 1024, 512
+P = 128
+PACK = 4
+HALF = 256
+FLOPS = 2 * K * M * S
+
+F32 = mybir.dt.float32
+BF16 = mybir.dt.bfloat16
+U32 = mybir.dt.uint32
+I32 = mybir.dt.int32
+U16 = mybir.dt.uint16
+U8 = mybir.dt.uint8
+FP8X4 = mybir.dt.float8_e4m3fn_x4
+MULT = mybir.AluOpType.mult
+
+
+def tile_list_hboth_none_kernel(tc, xT, w_words, w_scales, wgt, wgo, offs, offs2, out):
+    nc = tc.nc
+    rows = M // P
+    with ExitStack() as ctx:
+        keep = ctx.enter_context(tc.tile_pool(name="keep", bufs=1))
+        psum = ctx.enter_context(tc.psum_pool(name="psum", bufs=1))
+
+        offs_sb = keep.tile([P, S // 16], U16, name="offs_sb")
+        offs2_sb = keep.tile([P, S // 16], U16, name="offs2_sb")
+        wgt_sb = keep.tile([P, S], F32, name="wgt_sb")
+        wgo_sb = keep.tile([P, S], F32, name="wgo_sb")
+        w_codes = keep.tile([P, M], U32, name="w_codes", align_bytes=64)
+        w_sc = keep.tile([P, M], U8, name="w_sc", align_bytes=64)
+        table = [keep.tile([P, T], F32, name="table%d" % i) for i in range(PACK)]
+        window = [keep.tile([P, T], F32, name="window%d" % b) for b in range(rows)]
+        picked = [keep.tile([P, PACK, HALF], F32, name="picked%d" % h) for h in range(2)]
+        grouped = [keep.tile([P, HALF, PACK], BF16, name="grouped%d" % h, align_bytes=64) for h in range(2)]
+        x_codes = [keep.tile([P, HALF], U32, name="x_codes%d" % h, align_bytes=64) for h in range(2)]
+        x_sc = [keep.tile([P, HALF], U8, name="x_sc%d" % h, align_bytes=64) for h in range(2)]
+        bank = [[psum.tile([P, HALF], F32, name="bank%d_%d" % (h, b)) for b in range(rows)] for h in range(2)]
+        y = [[keep.tile([P, HALF], F32, name="y%d_%d" % (h, b)) for b in range(rows)] for h in range(2)]
+
+        x_planes = xT.rearrange("(p i) t -> i p t", i=PACK)
+        lo, hi = slice(0, HALF), slice(HALF, S)
+        cols = [lo, hi]
+        lists = [slice(0, HALF // 16), slice(HALF // 16, S // 16)]
+
+        nc.sync.dma_start(offs_sb[:], offs)
+        nc.sync.dma_start(wgt_sb[:, lo], wgt[:, lo])
+        nc.sync.dma_start(table[0][:], x_planes[0])
+        nc.sync.dma_start(wgt_sb[:, hi], wgt[:, hi])
+        for i in range(1, PACK):
+            nc.sync.dma_start(table[i][:], x_planes[i])
+        nc.gpsimd.memset(w_sc[:].bitcast(I32), 0)
+        for q in range(4):
+            nc.sync.dma_start(w_sc[32 * q : 32 * q + 4, :].bitcast(I32), w_scales[0, 4 * q : 4 * q + 4, :].bitcast(I32))
+        nc.sync.dma_start(w_codes[:].bitcast(I32), w_words[0].rearrange("p n i -> p (n i)").bitcast(I32))
+        nc.sync.dma_start(offs2_sb[:], offs2)
+        nc.sync.dma_start(wgo_sb[:], wgo)
+
+        for b in range(rows):
+            nc.vector.memset(window[b][:], 0.0)
+
+        def gather(h, i, first=0, last=HALF):
+            start = h * HALF
+            nc.vector.tensor_tensor(
+                picked[h][:, i, first:last],
+                table[i][:].indirect(offs_sb[:, (start + first) // 16 : (start + last) // 16]),
+                wgt_sb[:, start + first : start + last],
+                MULT,
+            )
+
+        def interleave(h, pair, first=0, last=HALF):
+            two = slice(2 * pair, 2 * pair + 2)
+            nc.scalar.copy(grouped[h][:, first:last, two], picked[h][:, two, first:last].rearrange("p i n -> p n i"))
+
+        def quantize(h):
+            nc.vector.quantize_mx(
+                out=x_codes[h][:].bitcast(FP8X4), scales=x_sc[h][:], in_=grouped[h][:].rearrange("p n i -> p (n i)")
+            )
+
+        def multiply(h, b):
+            m = slice(P * b, P * b + P)
+            nc.tensor.matmul_mx(
+                out=bank[h][b][:],
+                lhsT=w_codes[:, m].bitcast(FP8X4),
+                lhsT_scale=w_sc[:, m],
+                rhs=x_codes[h][:].bitcast(FP8X4),
+                rhs_scale=x_sc[h][:],
+                start=True,
+                stop=True,
+            )
+
+        def empty(h, b):
+            nc.scalar.copy(y[h][b][:], bank[h][b][:])
+
+        def scatter(h, b):
+            nc.vector.tensor_tensor(window[b][:].indirect(offs2_sb[:, lists[h]]), y[h][b][:], wgo_sb[:, cols[h]], MULT)
+
+        gather(0, 0)
+        gather(1, 0)
+        gather(0, 1)
+        interleave(0, 0)
+        gather(1, 1)
+        interleave(1, 0)
+        gather(0, 2)
+        for first in range(0, HALF, P):
+            gather(0, 3, first, first + P)
+            interleave(0, 1, first, first + P)
+        gather(1, 2)
+        quantize(0)
+        for b in range(rows):
+            multiply(0, b)
+        empty(0, 0)
+        gather(1, 3)
+        interleave(1, 1)
+        scatter(0, 0)
+        quantize(1)
+        for b in range(1, rows):
+            empty(0, b)
+            scatter(0, b)
+        for b in range(rows):
+            multiply(1, b)
+            empty(1, b)
+            scatter(1, b)
+            nc.sync.dma_start(out[P * b : P * b + P, :], window[b][:])

@@ -32,8 +32,8 @@ def tile_list_hboth_none_kernel(tc, xT, w_words, w_scales, wgt, wgo, offs, offs2
         w_codes = keep.tile([P, M], U32, name="w_codes", align_bytes=64)
         w_sc = keep.tile([P, M], U8, name="w_sc", align_bytes=64)
         table = [keep.tile([P, T], F32, name="table%d" % i) for i in range(PACK)]
-        window = [keep.tile([P, T], F32, name="window%d" % b) for b in range(rows)]
-        picked = [keep.tile([P, PACK, HALF], F32, name="picked%d" % h) for h in range(2)]
+        window = [keep.tile([P, T], F32, name="window%d" % b) for b in range(rows - 1)]
+        early = [keep.tile([P, 2, HALF], F32, name="early%d" % h) for h in range(2)]
         grouped = [keep.tile([P, HALF, PACK], BF16, name="grouped%d" % h, align_bytes=64) for h in range(2)]
         x_codes = [keep.tile([P, HALF], U32, name="x_codes%d" % h, align_bytes=64) for h in range(2)]
         x_sc = [keep.tile([P, HALF], U8, name="x_sc%d" % h, align_bytes=64) for h in range(2)]
@@ -45,34 +45,34 @@ def tile_list_hboth_none_kernel(tc, xT, w_words, w_scales, wgt, wgo, offs, offs2
         cols = [lo, hi]
         lists = [slice(0, HALF // 16), slice(HALF // 16, S // 16)]
 
+        nc.sync.dma_start(table[0][:], x_planes[0])
         nc.sync.dma_start(offs_sb[:], offs)
         nc.sync.dma_start(wgt_sb[:, lo], wgt[:, lo])
-        nc.sync.dma_start(table[0][:], x_planes[0])
         nc.sync.dma_start(wgt_sb[:, hi], wgt[:, hi])
         for i in range(1, PACK):
             nc.sync.dma_start(table[i][:], x_planes[i])
-        nc.gpsimd.memset(w_sc[:].bitcast(I32), 0)
-        for q in range(4):
-            nc.sync.dma_start(w_sc[32 * q : 32 * q + 4, :].bitcast(I32), w_scales[0, 4 * q : 4 * q + 4, :].bitcast(I32))
         nc.sync.dma_start(w_codes[:].bitcast(I32), w_words[0].rearrange("p n i -> p (n i)").bitcast(I32))
         nc.sync.dma_start(offs2_sb[:], offs2)
         nc.sync.dma_start(wgo_sb[:], wgo)
 
-        for b in range(rows):
+        nc.vector.memset(w_sc[:].bitcast(I32), 0)
+        for q in range(4):
+            nc.gpsimd.dma_start(w_sc[32 * q : 32 * q + 4, :].bitcast(I32), w_scales[0, 4 * q : 4 * q + 4, :].bitcast(I32))
+        for b in range(rows - 1):
             nc.vector.memset(window[b][:], 0.0)
 
-        def gather(h, i, first=0, last=HALF):
+        def gather(result, h, i, first=0, last=HALF):
             start = h * HALF
             nc.vector.tensor_tensor(
-                picked[h][:, i, first:last],
+                result,
                 table[i][:].indirect(offs_sb[:, (start + first) // 16 : (start + last) // 16]),
                 wgt_sb[:, start + first : start + last],
                 MULT,
             )
 
-        def interleave(h, pair, first=0, last=HALF):
-            two = slice(2 * pair, 2 * pair + 2)
-            nc.scalar.copy(grouped[h][:, first:last, two], picked[h][:, two, first:last].rearrange("p i n -> p n i"))
+        def interleave(h, i, source, first=0, last=HALF):
+            count = source.shape[1]
+            nc.scalar.copy(grouped[h][:, first:last, i : i + count], source.rearrange("p i n -> p n i"))
 
         def quantize(h):
             nc.vector.quantize_mx(
@@ -97,27 +97,32 @@ def tile_list_hboth_none_kernel(tc, xT, w_words, w_scales, wgt, wgo, offs, offs2
         def scatter(h, b):
             nc.vector.tensor_tensor(window[b][:].indirect(offs2_sb[:, lists[h]]), y[h][b][:], wgo_sb[:, cols[h]], MULT)
 
-        gather(0, 0)
-        gather(1, 0)
-        gather(0, 1)
-        interleave(0, 0)
-        gather(1, 1)
-        interleave(1, 0)
-        gather(0, 2)
+        for i in range(2):
+            for h in range(2):
+                gather(early[h][:, i, :], h, i)
+        for h in range(2):
+            interleave(h, 0, early[h][:])
+        late = keep.tile([P, 2, HALF], F32, name="late0")
+        gather(late[:, 0, :], 0, 2)
         for first in range(0, HALF, P):
-            gather(0, 3, first, first + P)
-            interleave(0, 1, first, first + P)
-        gather(1, 2)
+            last = first + P
+            gather(late[:, 1, first:last], 0, 3, first, last)
+            interleave(0, 2, late[:, :, first:last], first, last)
         quantize(0)
         for b in range(rows):
             multiply(0, b)
-        empty(0, 0)
-        gather(1, 3)
-        interleave(1, 1)
+            empty(0, b)
+        window.append(keep.tile([P, T], F32, name="window3", tag="table0"))
+        nc.gpsimd.memset(window[rows - 1][:], 0.0)
+        plane2 = keep.tile([P, 1, HALF], F32, name="plane2")
+        gather(plane2[:, 0, :], 1, 2)
+        interleave(1, 2, plane2[:])
+        plane3 = keep.tile([P, 1, HALF], F32, name="plane3")
+        gather(plane3[:, 0, :], 1, 3)
+        interleave(1, 3, plane3[:])
         scatter(0, 0)
         quantize(1)
         for b in range(1, rows):
-            empty(0, b)
             scatter(0, b)
         for b in range(rows):
             multiply(1, b)

from contextlib import ExitStack

import concourse.mybir as mybir

K, M, T, S = 512, 512, 1024, 512
P = 128
PACK = 4
HALF = 256
FLOPS = 2 * K * M * S

F32 = mybir.dt.float32
BF16 = mybir.dt.bfloat16
U32 = mybir.dt.uint32
I32 = mybir.dt.int32
U16 = mybir.dt.uint16
U8 = mybir.dt.uint8
FP8X4 = mybir.dt.float8_e4m3fn_x4
MULT = mybir.AluOpType.mult


def tile_list_hboth_none_kernel(tc, xT, w_words, w_scales, wgt, wgo, offs, offs2, out):
    nc = tc.nc
    rows = M // P
    with ExitStack() as ctx:
        keep = ctx.enter_context(tc.tile_pool(name="keep", bufs=1))
        psum = ctx.enter_context(tc.psum_pool(name="psum", bufs=1))

        offs_sb = keep.tile([P, S // 16], U16, name="offs_sb")
        offs2_sb = keep.tile([P, S // 16], U16, name="offs2_sb")
        wgt_sb = keep.tile([P, S], F32, name="wgt_sb")
        wgo_sb = keep.tile([P, S], F32, name="wgo_sb")
        w_codes = keep.tile([P, M], U32, name="w_codes", align_bytes=64)
        w_sc = keep.tile([P, M], U8, name="w_sc", align_bytes=64)
        table = [keep.tile([P, T], F32, name="table%d" % i) for i in range(PACK)]
        window = [keep.tile([P, T], F32, name="window%d" % b) for b in range(rows - 1)]
        early = [keep.tile([P, 2, HALF], F32, name="early%d" % h) for h in range(2)]
        grouped = [keep.tile([P, HALF, PACK], BF16, name="grouped%d" % h, align_bytes=64) for h in range(2)]
        x_codes = [keep.tile([P, HALF], U32, name="x_codes%d" % h, align_bytes=64) for h in range(2)]
        x_sc = [keep.tile([P, HALF], U8, name="x_sc%d" % h, align_bytes=64) for h in range(2)]
        bank = [[psum.tile([P, HALF], F32, name="bank%d_%d" % (h, b)) for b in range(rows)] for h in range(2)]
        y = [[keep.tile([P, HALF], F32, name="y%d_%d" % (h, b)) for b in range(rows)] for h in range(2)]

        x_planes = xT.rearrange("(p i) t -> i p t", i=PACK)
        lo, hi = slice(0, HALF), slice(HALF, S)
        cols = [lo, hi]
        lists = [slice(0, HALF // 16), slice(HALF // 16, S // 16)]

        nc.sync.dma_start(table[0][:], x_planes[0])
        nc.sync.dma_start(offs_sb[:], offs)
        nc.sync.dma_start(wgt_sb[:, lo], wgt[:, lo])
        nc.sync.dma_start(wgt_sb[:, hi], wgt[:, hi])
        for i in range(1, PACK):
            nc.sync.dma_start(table[i][:], x_planes[i])
        nc.sync.dma_start(w_codes[:].bitcast(I32), w_words[0].rearrange("p n i -> p (n i)").bitcast(I32))
        nc.sync.dma_start(offs2_sb[:], offs2)
        nc.sync.dma_start(wgo_sb[:], wgo)

        nc.vector.memset(w_sc[:].bitcast(I32), 0)
        for q in range(4):
            nc.gpsimd.dma_start(w_sc[32 * q : 32 * q + 4, :].bitcast(I32), w_scales[0, 4 * q : 4 * q + 4, :].bitcast(I32))
        for b in range(rows - 1):
            nc.vector.memset(window[b][:], 0.0)

        def gather(result, h, i, first=0, last=HALF):
            start = h * HALF
            nc.vector.tensor_tensor(
                result,
                table[i][:].indirect(offs_sb[:, (start + first) // 16 : (start + last) // 16]),
                wgt_sb[:, start + first : start + last],
                MULT,
            )

        def interleave(h, i, source, first=0, last=HALF):
            count = source.shape[1]
            nc.scalar.copy(grouped[h][:, first:last, i : i + count], source.rearrange("p i n -> p n i"))

        def quantize(h):
            nc.vector.quantize_mx(
                out=x_codes[h][:].bitcast(FP8X4), scales=x_sc[h][:], in_=grouped[h][:].rearrange("p n i -> p (n i)")
            )

        def multiply(h, b):
            m = slice(P * b, P * b + P)
            nc.tensor.matmul_mx(
                out=bank[h][b][:],
                lhsT=w_codes[:, m].bitcast(FP8X4),
                lhsT_scale=w_sc[:, m],
                rhs=x_codes[h][:].bitcast(FP8X4),
                rhs_scale=x_sc[h][:],
                start=True,
                stop=True,
            )

        def empty(h, b):
            nc.scalar.copy(y[h][b][:], bank[h][b][:])

        def scatter(h, b):
            nc.vector.tensor_tensor(window[b][:].indirect(offs2_sb[:, lists[h]]), y[h][b][:], wgo_sb[:, cols[h]], MULT)

        for i in range(2):
            for h in range(2):
                gather(early[h][:, i, :], h, i)
        for h in range(2):
            interleave(h, 0, early[h][:])
        late = keep.tile([P, 2, HALF], F32, name="late0")
        gather(late[:, 0, :], 0, 2)
        for first in range(0, HALF, P):
            last = first + P
            gather(late[:, 1, first:last], 0, 3, first, last)
            interleave(0, 2, late[:, :, first:last], first, last)
        quantize(0)
        for b in range(rows):
            multiply(0, b)
            empty(0, b)
        window.append(keep.tile([P, T], F32, name="window3", tag="table0"))
        nc.gpsimd.memset(window[rows - 1][:], 0.0)
        plane2 = keep.tile([P, 1, HALF], F32, name="plane2")
        gather(plane2[:, 0, :], 1, 2)
        interleave(1, 2, plane2[:])
        plane3 = keep.tile([P, 1, HALF], F32, name="plane3")
        gather(plane3[:, 0, :], 1, 3)
        interleave(1, 3, plane3[:])
        scatter(0, 0)
        quantize(1)
        for b in range(1, rows):
            scatter(0, b)
        for b in range(rows):
            multiply(1, b)
            empty(1, b)
            scatter(1, b)
            nc.sync.dma_start(out[P * b : P * b + P, :], window[b][:])
